import numpy as np
import ml_dtypes


def mxq(x, axis, fmt="e4m3"):
    dtype, down = {"e4m3": (ml_dtypes.float8_e4m3fn, 7), "e5m2": (ml_dtypes.float8_e5m2, 14)}[fmt]
    v = np.moveaxis(np.asarray(x, np.float32).astype(ml_dtypes.bfloat16).astype(np.float64), axis, -1)
    blocks = v.reshape(v.shape[:-1] + (-1, 32))
    amax = np.abs(blocks).max(-1, keepdims=True)
    byte = np.maximum(np.where(amax > 0, np.frexp(amax)[1] - 1 + 127, 0) - down, 1)
    scale = np.exp2(byte - 127.0)
    codes = (blocks / scale).astype(np.float32).astype(dtype).astype(np.float64)
    return np.moveaxis((codes * scale).reshape(v.shape), -1, axis)


WIDE = False


def mx_kscale(k):
    if not WIDE:
        return np.ones(k)
    levels = np.array([10, -10, 5, -5, 0])
    if k % 512:
        return np.exp2(np.random.permutation(np.resize(levels, k // 32))).repeat(32)
    a = np.empty((k // 512, 16))
    for p in range(k // 512):
        a[p, :8] = np.random.permutation(np.resize(levels, 8))
        for g in range(8):
            far = levels[np.abs(levels - a[p, g]) >= 10]
            a[p, g + 8] = far[np.random.randint(len(far))]
    return np.exp2(a.ravel()).repeat(32)


def f64(x):
    return np.asarray(x).astype(np.float64)


def striped(idx):
    return np.tile(idx.reshape(-1, 16).T, (8, 1)).astype(np.uint16)


def unstriped(offs):
    return offs[:16].T.reshape(-1).astype(np.int64)


def pack_weight(w):
    k, n = w.shape
    w = f64(np.asarray(w, np.float32).astype(ml_dtypes.bfloat16)).reshape(k // 32, 32, n)
    amax = np.abs(w).max(1)
    byte = np.clip(np.where(amax > 0, np.frexp(amax)[1] - 1 + 127 - 7, 1), 1, 254)
    scaled = (w * np.exp2(127.0 - byte)[:, None, :]).reshape(k, n).astype(np.float32)
    words = np.ascontiguousarray(scaled.reshape(k // 512, 128, 4, n).transpose(0, 1, 3, 2)).astype(ml_dtypes.float8_e4m3fn).view(np.uint8)
    return words, np.ascontiguousarray(byte.astype(np.uint8).reshape(k // 512, 16, n))


def unpack_weight(words, scales):
    g, p, n, _ = words.shape
    vals = np.ascontiguousarray(words).view(ml_dtypes.float8_e4m3fn).astype(np.float64) * np.repeat(np.exp2(scales.astype(np.float64) - 127.0), 8, axis=1)[..., None]
    return vals.transpose(0, 1, 3, 2).reshape(g * 512, n)


def relu(v):
    return np.maximum(v, 0.0)


K, T, S, H, V = 512, 1024, 512, 512, 256
P = 2 ** 7


def setup_inputs():
    n = np.random.standard_normal
    s = mx_kscale(K)[:, None]
    u = mx_kscale(H)
    packed_xT = pack_weight(n((K, T)) * s)
    return {
        "x_words": packed_xT[0],
        "x_scales": packed_xT[1],
        "w1": (n((K, H)) / np.sqrt(K) / s * u).astype(np.float32),
        "wk": (n((H, V)) / np.sqrt(H) / u[:, None]).astype(np.float32),
        "knot": (np.tile(np.arange(V) / V, (P, 1))).astype(np.float32),
        "thr": (np.random.uniform(0.2, 1.0, (S, 1))).astype(np.float32),
        "full": (np.tile(np.ones(V) * np.random.uniform(0.9, 1.0, V), (P, 1))).astype(np.float32),
        "offs": striped(np.random.permutation(T)[:S]),
    }


def reference(x_words, x_scales, w1, wk, knot, thr, full, offs):
    xq = unpack_weight(x_words, x_scales)[:, unstriped(offs)]
    h = relu(mxq(f64(w1), 0, "e4m3").T @ xq)
    wkq = mxq(f64(wk), 0, "e4m3")
    a = np.log(np.exp(mxq(h, 0, "e4m3").T @ wkq) + 1.0)
    rr = np.minimum(relu(256.0 * (-1.0 * f64(knot)[:1] + f64(thr))), f64(full)[:1])
    p = a * rr
    total = p.sum(axis=1, keepdims=True) + 1.0
    return np.log(100.0 * (p / total) + 0.1)

@@ -1,0 +1,152 @@
+import math
+from contextlib import ExitStack
+
+import concourse.mybir as mybir
+
+F32 = mybir.dt.float32
+BF16 = mybir.dt.bfloat16
+I32 = mybir.dt.int32
+U32 = mybir.dt.uint32
+U16 = mybir.dt.uint16
+U8 = mybir.dt.uint8
+FP8X4 = mybir.dt.float8_e4m3fn_x4
+ALU = mybir.AluOpType
+ACT = mybir.ActivationFunctionType
+
+P = 128
+PACK = 4
+K, T, S, H, V = 512, 1024, 512, 512, 256
+TILES = S // P
+CAP = 32.0
+FLOPS = 2 * K * H * S + 2 * H * S * V
+
+
+def tile_picked_ycard_log_p_kernel(tc, x_words, x_scales, w1, wk, knot, thr, full, offs, out):
+    nc = tc.nc
+    with ExitStack() as ctx:
+        sb = ctx.enter_context(tc.tile_pool(name="sb", bufs=1))
+        ps = ctx.enter_context(tc.psum_pool(name="ps", bufs=1))
+
+        offsets = sb.tile([P, S // 16], U16, name="offsets")
+        nc.sync.dma_start(offsets[:], offs)
+
+        xs_all = sb.tile([P, T], U8, name="xs_all", align_bytes=64)
+        nc.vector.memset(xs_all[:].bitcast(I32), 0)
+        for q in range(4):
+            nc.scalar.dma_start(xs_all[32 * q : 32 * q + 4, :].bitcast(I32), x_scales[0, 4 * q : 4 * q + 4, :].bitcast(I32))
+
+        xw_all = sb.tile([P, T], I32, name="xw_all", align_bytes=64)
+        nc.sync.dma_start(xw_all[:], x_words[0].rearrange("p n t -> p (n t)").bitcast(I32))
+
+        w1_rows = w1.rearrange("(p j) c -> p j c", j=PACK)
+        w1_raw = []
+        for half in range(2):
+            raw = sb.tile([P, PACK, H // 2], F32, name="w1_raw%d" % half, align_bytes=64)
+            nc.sync.dma_start(raw[:], w1_rows[:, :, half * (H // 2) : (half + 1) * (H // 2)])
+            w1_raw.append(raw)
+        wk_raw = sb.tile([P, PACK, V], F32, name="wk_raw", align_bytes=64)
+        nc.sync.dma_start(wk_raw[:], wk.rearrange("(p j) c -> p j c", j=PACK))
+        knot_sb = sb.tile([P, V], F32, name="knot_sb")
+        nc.sync.dma_start(knot_sb[:], knot)
+        thr_sb = sb.tile([P, TILES], F32, name="thr_sb")
+        with nc.allow_non_contiguous_dma(reason="one threshold for each partition and token tile"):
+            nc.sync.dma_start(thr_sb[:], thr.rearrange("(c p) o -> p (c o)", p=P))
+        full_sb = sb.tile([P, V], F32, name="full_sb")
+        nc.sync.dma_start(full_sb[:], full)
+
+        xs = sb.tile([P, S], U8, name="xs", align_bytes=64)
+        xw = sb.tile([P, S], U32, name="xw", align_bytes=64)
+        nc.vector.tensor_copy(xs[:], xs_all[:].indirect(offsets[:]))
+        nc.vector.tensor_copy(xw[:], xw_all[:].bitcast(U32).indirect(offsets[:]))
+
+        w1_bf = sb.tile([P, PACK, P, PACK], BF16, name="w1_bf", align_bytes=64)
+        half_m = P // 2
+        nc.scalar.activation(
+            w1_bf[:, :, 0:half_m, :].rearrange("p t m j -> p m j t"),
+            w1_raw[0][:].rearrange("p j (m t) -> p m j t", t=PACK),
+            ACT.Copy,
+        )
+        nc.vector.tensor_copy(
+            w1_bf[:, :, half_m:P, :].rearrange("p t m j -> p m j t"),
+            w1_raw[1][:].rearrange("p j (m t) -> p m j t", t=PACK),
+        )
+        w1_q = sb.tile([P, H], U32, name="w1_q", align_bytes=64)
+        w1_s = sb.tile([P, H], U8, name="w1_s", align_bytes=64)
+        for pair in range(2):
+            cols = slice(pair * 2 * P, (pair + 1) * 2 * P)
+            nc.vector.quantize_mx(
+                w1_q[:, cols].bitcast(FP8X4),
+                w1_s[:, cols],
+                w1_bf[:, 2 * pair : 2 * pair + 2, :, :].rearrange("p t m j -> p (t m j)"),
+            )
+
+        wk_bf = sb.tile([P, V, PACK], BF16, name="wk_bf", align_bytes=64)
+        nc.vector.tensor_copy(
+            wk_bf[:].rearrange("p (c i) j -> p c j i", i=PACK),
+            wk_raw[:].rearrange("p j (c i) -> p c j i", i=PACK),
+        )
+        wk_q = sb.tile([P, V], U32, name="wk_q", align_bytes=64)
+        wk_s = sb.tile([P, V], U8, name="wk_s", align_bytes=64)
+        nc.vector.quantize_mx(wk_q[:].bitcast(FP8X4), wk_s[:], wk_bf[:].rearrange("p c j -> p (c j)"))
+
+        h_ps = []
+        for c in range(TILES):
+            bank = ps.tile([P, PACK, P], F32, name="h_ps%d" % c)
+            tok = slice(c * P, (c + 1) * P)
+            for t in range(PACK):
+                cols = slice(t * P, (t + 1) * P)
+                nc.tensor.matmul_mx(
+                    bank[:, t, :], lhsT=w1_q[:, cols].bitcast(FP8X4), lhsT_scale=w1_s[:, cols],
+                    rhs=xw[:, tok].bitcast(FP8X4), rhs_scale=xs[:, tok], start=True, stop=True,
+                )
+            h_ps.append(bank)
+
+        grown = sb.tile([P, TILES, V], F32, name="grown")
+        z_ps = []
+        for c in range(TILES):
+            h_bf = sb.tile([P, P, PACK], BF16, name="h_bf%d" % c, align_bytes=64)
+            if c % 2 == 0:
+                nc.scalar.activation(h_bf[:], h_ps[c][:].rearrange("p t n -> p n t"), ACT.Relu)
+            else:
+                nc.vector.tensor_scalar(h_bf[:], h_ps[c][:].rearrange("p t n -> p n t"), 0.0, None, ALU.max)
+            h_q = sb.tile([P, P], U32, name="h_q%d" % c, align_bytes=64)
+            h_s = sb.tile([P, P], U8, name="h_s%d" % c, align_bytes=64)
+            nc.vector.quantize_mx(h_q[:].bitcast(FP8X4), h_s[:], h_bf[:].rearrange("p n t -> p (n t)"))
+            z = ps.tile([P, V], F32, name="z_ps%d" % c)
+            nc.tensor.matmul_mx(
+                z[:], lhsT=h_q[:].bitcast(FP8X4), lhsT_scale=h_s[:],
+                rhs=wk_q[:].bitcast(FP8X4), rhs_scale=wk_s[:], start=True, stop=True,
+            )
+            nc.scalar.activation(grown[:, c, :], z[:], ACT.Exp)
+            z_ps.append(z)
+
+        capped = sb.tile([P, TILES, V], F32, name="capped")
+        nc.vector.tensor_scalar(capped[:], grown[:], math.e**CAP, None, ALU.min)
+
+        reach = []
+        for c in range(TILES):
+            above = sb.tile([P, V], F32, name="above%d" % c)
+            nc.scalar.activation(above[:], knot_sb[:], ACT.Relu, bias=thr_sb[:, c : c + 1], scale=-1.0)
+            rr = sb.tile([P, V], F32, name="rr%d" % c)
+            nc.vector.scalar_tensor_tensor(rr[:], above[:], 256.0, full_sb[:], ALU.mult, ALU.min)
+            weight = sb.tile([P, V], F32, name="weight%d" % c)
+            nc.vector.scalar_tensor_tensor(weight[:], z_ps[c][:], CAP, rr[:], ALU.max, ALU.mult)
+            reach.append(weight)
+
+        soft = []
+        for c in range(TILES):
+            a = sb.tile([P, V], F32, name="soft%d" % c)
+            nc.scalar.activation(a[:], capped[:, c, :], ACT.Ln, bias=1.0)
+            soft.append(a)
+
+        for c in range(TILES):
+            piece = sb.tile([P, V], F32, name="piece%d" % c)
+            sums = sb.tile([P, 1], F32, name="sums%d" % c)
+            nc.vector.scalar_tensor_tensor(piece[:], soft[c][:], 1.0, reach[c][:], ALU.mult, ALU.mult, accum_out=sums[:])
+            total = sb.tile([P, 1], F32, name="total%d" % c)
+            nc.vector.tensor_scalar(total[:], sums[:], CAP, 0.01, ALU.add, ALU.mult)
+            factor = sb.tile([P, 1], F32, name="factor%d" % c)
+            nc.vector.reciprocal(factor[:], total[:])
+            res = sb.tile([P, V], F32, name="res%d" % c)
+            nc.scalar.activation(res[:], piece[:], ACT.Ln, bias=0.1, scale=factor[:])
+            nc.sync.dma_start(out[c * P : (c + 1) * P, :], res[:])

@@ -2,6 +2,7 @@ import math
 from contextlib import ExitStack
 
 import concourse.mybir as mybir
+from concourse.masks import make_identity
 
 F32 = mybir.dt.float32
 BF16 = mybir.dt.bfloat16
@@ -18,6 +19,7 @@ PACK = 4
 K, T, S, H, V = 512, 1024, 512, 512, 256
 TILES = S // P
 CAP = 32.0
+W1_SPLIT = 44
 FLOPS = 2 * K * H * S + 2 * H * S * V
 
 
@@ -31,56 +33,52 @@ def tile_picked_ycard_log_p_kernel(tc, x_words, x_scales, w1, wk, knot, thr, ful
         nc.sync.dma_start(offsets[:], offs)
 
         xs_all = sb.tile([P, T], U8, name="xs_all", align_bytes=64)
-        nc.vector.memset(xs_all[:].bitcast(I32), 0)
-        for q in range(4):
-            nc.scalar.dma_start(xs_all[32 * q : 32 * q + 4, :].bitcast(I32), x_scales[0, 4 * q : 4 * q + 4, :].bitcast(I32))
+        nc.gpsimd.memset(xs_all[:].bitcast(I32), 0)
+        thr_rows = sb.tile([P, P], F32, name="thr_rows")
+        nc.gpsimd.memset(thr_rows[:], 0.0)
+        identity = sb.tile([P, P], F32, name="identity")
+        make_identity(nc, identity[:])
 
         xw_all = sb.tile([P, T], I32, name="xw_all", align_bytes=64)
         nc.sync.dma_start(xw_all[:], x_words[0].rearrange("p n t -> p (n t)").bitcast(I32))
-
-        w1_rows = w1.rearrange("(p j) c -> p j c", j=PACK)
-        w1_raw = []
-        for half in range(2):
-            raw = sb.tile([P, PACK, H // 2], F32, name="w1_raw%d" % half, align_bytes=64)
-            nc.sync.dma_start(raw[:], w1_rows[:, :, half * (H // 2) : (half + 1) * (H // 2)])
-            w1_raw.append(raw)
-        wk_raw = sb.tile([P, PACK, V], F32, name="wk_raw", align_bytes=64)
-        nc.sync.dma_start(wk_raw[:], wk.rearrange("(p j) c -> p j c", j=PACK))
+        for q in range(4):
+            nc.sync.dma_start(xs_all[32 * q : 32 * q + 4, :].bitcast(I32), x_scales[0, 4 * q : 4 * q + 4, :].bitcast(I32))
+        nc.sync.dma_start(thr_rows[0:TILES, :], thr.rearrange("(c p) o -> c (p o)", p=P))
+        w1_raw = sb.tile([P, PACK, H], F32, name="w1_raw", tag="first_in", align_bytes=64)
+        nc.sync.dma_start(w1_raw[:], w1.rearrange("(p j) c -> p j c", j=PACK))
         knot_sb = sb.tile([P, V], F32, name="knot_sb")
         nc.sync.dma_start(knot_sb[:], knot)
-        thr_sb = sb.tile([P, TILES], F32, name="thr_sb")
-        with nc.allow_non_contiguous_dma(reason="one threshold for each partition and token tile"):
-            nc.sync.dma_start(thr_sb[:], thr.rearrange("(c p) o -> p (c o)", p=P))
+        wk_raw = sb.tile([P, PACK, V], F32, name="wk_raw", tag="codes0", align_bytes=64)
+        nc.sync.dma_start(wk_raw[:], wk.rearrange("(p j) c -> p j c", j=PACK))
         full_sb = sb.tile([P, V], F32, name="full_sb")
         nc.sync.dma_start(full_sb[:], full)
 
         xs = sb.tile([P, S], U8, name="xs", align_bytes=64)
         xw = sb.tile([P, S], U32, name="xw", align_bytes=64)
-        nc.vector.tensor_copy(xs[:], xs_all[:].indirect(offsets[:]))
         nc.vector.tensor_copy(xw[:], xw_all[:].bitcast(U32).indirect(offsets[:]))
+        nc.vector.tensor_copy(xs[:], xs_all[:].indirect(offsets[:]))
 
-        w1_bf = sb.tile([P, PACK, P, PACK], BF16, name="w1_bf", align_bytes=64)
-        half_m = P // 2
-        nc.scalar.activation(
-            w1_bf[:, :, 0:half_m, :].rearrange("p t m j -> p m j t"),
-            w1_raw[0][:].rearrange("p j (m t) -> p m j t", t=PACK),
-            ACT.Copy,
-        )
-        nc.vector.tensor_copy(
-            w1_bf[:, :, half_m:P, :].rearrange("p t m j -> p m j t"),
-            w1_raw[1][:].rearrange("p j (m t) -> p m j t", t=PACK),
-        )
+        thr_ps = ps.tile([P, P], F32, name="thr_ps", tag="z_ps%d" % (TILES - 1))
+        nc.tensor.transpose(thr_ps[:], thr_rows[:], identity[:])
+        thr_cols = sb.tile([P, TILES], F32, name="thr_cols")
+        nc.scalar.activation(thr_cols[:], thr_ps[:, 0:TILES], ACT.Copy, scale=256.0)
+
+        w1_bf = sb.tile([P, PACK, P, PACK], BF16, name="w1_bf", tag="stage%d" % (TILES - 1), align_bytes=64)
+        dealt = w1_bf[:].rearrange("p t m j -> p m j t")
+        rows = w1_raw[:].rearrange("p j (m t) -> p m j t", t=PACK)
+        nc.scalar.activation(dealt[:, 0:W1_SPLIT], rows[:, 0:W1_SPLIT], ACT.Copy)
+        nc.vector.tensor_copy(dealt[:, W1_SPLIT:P], rows[:, W1_SPLIT:P])
         w1_q = sb.tile([P, H], U32, name="w1_q", align_bytes=64)
         w1_s = sb.tile([P, H], U8, name="w1_s", align_bytes=64)
-        for pair in range(2):
-            cols = slice(pair * 2 * P, (pair + 1) * 2 * P)
-            nc.vector.quantize_mx(
-                w1_q[:, cols].bitcast(FP8X4),
-                w1_s[:, cols],
-                w1_bf[:, 2 * pair : 2 * pair + 2, :, :].rearrange("p t m j -> p (t m j)"),
-            )
+        for t in range(PACK):
+            cols = slice(t * P, (t + 1) * P)
+            nc.vector.quantize_mx(w1_q[:, cols].bitcast(FP8X4), w1_s[:, cols], w1_bf[:, t, :, :].rearrange("p m j -> p (m j)"))
 
-        wk_bf = sb.tile([P, V, PACK], BF16, name="wk_bf", align_bytes=64)
+        above = sb.tile([P, TILES, V], F32, name="above", tag="first_in", align_bytes=64)
+        for c in range(TILES):
+            nc.scalar.activation(above[:, c, :], knot_sb[:], ACT.Relu, bias=thr_cols[:, c : c + 1], scale=-256.0)
+
+        wk_bf = sb.tile([P, V, PACK], BF16, name="wk_bf", tag="stage%d" % (TILES - 1), align_bytes=64)
         nc.vector.tensor_copy(
             wk_bf[:].rearrange("p (c i) j -> p c j i", i=PACK),
             wk_raw[:].rearrange("p j (c i) -> p c j i", i=PACK),
@@ -104,15 +102,15 @@ def tile_picked_ycard_log_p_kernel(tc, x_words, x_scales, w1, wk, knot, thr, ful
         grown = sb.tile([P, TILES, V], F32, name="grown")
         z_ps = []
         for c in range(TILES):
-            h_bf = sb.tile([P, P, PACK], BF16, name="h_bf%d" % c, align_bytes=64)
-            if c % 2 == 0:
+            h_bf = sb.tile([P, P, PACK], BF16, name="h_bf%d" % c, tag="stage%d" % c, align_bytes=64)
+            if c < TILES - 1:
                 nc.scalar.activation(h_bf[:], h_ps[c][:].rearrange("p t n -> p n t"), ACT.Relu)
             else:
                 nc.vector.tensor_scalar(h_bf[:], h_ps[c][:].rearrange("p t n -> p n t"), 0.0, None, ALU.max)
-            h_q = sb.tile([P, P], U32, name="h_q%d" % c, align_bytes=64)
+            h_q = sb.tile([P, P], U32, name="h_q%d" % c, tag="codes%d" % c, align_bytes=64)
             h_s = sb.tile([P, P], U8, name="h_s%d" % c, align_bytes=64)
             nc.vector.quantize_mx(h_q[:].bitcast(FP8X4), h_s[:], h_bf[:].rearrange("p n t -> p (n t)"))
-            z = ps.tile([P, V], F32, name="z_ps%d" % c)
+            z = ps.tile([P, V], F32, name="z_ps%d" % c, tag="z_ps%d" % c)
             nc.tensor.matmul_mx(
                 z[:], lhsT=h_q[:].bitcast(FP8X4), lhsT_scale=h_s[:],
                 rhs=wk_q[:].bitcast(FP8X4), rhs_scale=wk_s[:], start=True, stop=True,
@@ -125,10 +123,8 @@ def tile_picked_ycard_log_p_kernel(tc, x_words, x_scales, w1, wk, knot, thr, ful
 
         reach = []
         for c in range(TILES):
-            above = sb.tile([P, V], F32, name="above%d" % c)
-            nc.scalar.activation(above[:], knot_sb[:], ACT.Relu, bias=thr_sb[:, c : c + 1], scale=-1.0)
-            rr = sb.tile([P, V], F32, name="rr%d" % c)
-            nc.vector.scalar_tensor_tensor(rr[:], above[:], 256.0, full_sb[:], ALU.mult, ALU.min)
+            rr = sb.tile([P, V], F32, name="rr%d" % c, tag="stage%d" % c, align_bytes=64)
+            nc.vector.tensor_tensor(rr[:], above[:, c, :], full_sb[:], ALU.min)
             weight = sb.tile([P, V], F32, name="weight%d" % c)
             nc.vector.scalar_tensor_tensor(weight[:], z_ps[c][:], CAP, rr[:], ALU.max, ALU.mult)
             reach.append(weight)

@@ -32,6 +32,11 @@ def tile_picked_ycard_log_p_kernel(tc, x_words, x_scales, w1, wk, knot, thr, ful
         offsets = sb.tile([P, S // 16], U16, name="offsets")
         nc.sync.dma_start(offsets[:], offs)
 
+        one = sb.tile([P, 1], F32, name="one")
+        nc.vector.memset(one[:], 1.0)
+        tenth = sb.tile([P, 1], F32, name="tenth")
+        nc.scalar.activation(tenth[:], one[:], ACT.Copy, scale=0.1)
+
         xs_all = sb.tile([P, T], U8, name="xs_all", align_bytes=64)
         nc.gpsimd.memset(xs_all[:].bitcast(I32), 0)
         thr_rows = sb.tile([P, P], F32, name="thr_rows")
@@ -39,13 +44,15 @@ def tile_picked_ycard_log_p_kernel(tc, x_words, x_scales, w1, wk, knot, thr, ful
         identity = sb.tile([P, P], F32, name="identity")
         make_identity(nc, identity[:])
 
-        xw_all = sb.tile([P, T], I32, name="xw_all", align_bytes=64)
-        nc.sync.dma_start(xw_all[:], x_words[0].rearrange("p n t -> p (n t)").bitcast(I32))
+        w1_raw = sb.tile([P, PACK, H], F32, name="w1_raw", tag="first_in", align_bytes=64)
+        w1_rows = w1.rearrange("(p j) c -> p j c", j=PACK)
+        nc.sync.dma_start(w1_raw[:, 0:2, :], w1_rows[:, 0:2, :])
         for q in range(4):
             nc.sync.dma_start(xs_all[32 * q : 32 * q + 4, :].bitcast(I32), x_scales[0, 4 * q : 4 * q + 4, :].bitcast(I32))
         nc.sync.dma_start(thr_rows[0:TILES, :], thr.rearrange("(c p) o -> c (p o)", p=P))
-        w1_raw = sb.tile([P, PACK, H], F32, name="w1_raw", tag="first_in", align_bytes=64)
-        nc.sync.dma_start(w1_raw[:], w1.rearrange("(p j) c -> p j c", j=PACK))
+        nc.sync.dma_start(w1_raw[:, 2:4, :], w1_rows[:, 2:4, :])
+        xw_all = sb.tile([P, T], I32, name="xw_all", align_bytes=64)
+        nc.sync.dma_start(xw_all[:], x_words[0].rearrange("p n t -> p (n t)").bitcast(I32))
         knot_sb = sb.tile([P, V], F32, name="knot_sb")
         nc.sync.dma_start(knot_sb[:], knot)
         wk_raw = sb.tile([P, PACK, V], F32, name="wk_raw", tag="codes0", align_bytes=64)
@@ -55,7 +62,6 @@ def tile_picked_ycard_log_p_kernel(tc, x_words, x_scales, w1, wk, knot, thr, ful
 
         xs = sb.tile([P, S], U8, name="xs", align_bytes=64)
         xw = sb.tile([P, S], U32, name="xw", align_bytes=64)
-        nc.vector.tensor_copy(xw[:], xw_all[:].bitcast(U32).indirect(offsets[:]))
         nc.vector.tensor_copy(xs[:], xs_all[:].indirect(offsets[:]))
 
         thr_ps = ps.tile([P, P], F32, name="thr_ps", tag="z_ps%d" % (TILES - 1))
@@ -63,7 +69,7 @@ def tile_picked_ycard_log_p_kernel(tc, x_words, x_scales, w1, wk, knot, thr, ful
         thr_cols = sb.tile([P, TILES], F32, name="thr_cols")
         nc.scalar.activation(thr_cols[:], thr_ps[:, 0:TILES], ACT.Copy, scale=256.0)
 
-        w1_bf = sb.tile([P, PACK, P, PACK], BF16, name="w1_bf", tag="stage%d" % (TILES - 1), align_bytes=64)
+        w1_bf = sb.tile([P, PACK, P, PACK], BF16, name="w1_bf", tag="weights_bf", align_bytes=64)
         dealt = w1_bf[:].rearrange("p t m j -> p m j t")
         rows = w1_raw[:].rearrange("p j (m t) -> p m j t", t=PACK)
         nc.scalar.activation(dealt[:, 0:W1_SPLIT], rows[:, 0:W1_SPLIT], ACT.Copy)
@@ -74,11 +80,15 @@ def tile_picked_ycard_log_p_kernel(tc, x_words, x_scales, w1, wk, knot, thr, ful
             cols = slice(t * P, (t + 1) * P)
             nc.vector.quantize_mx(w1_q[:, cols].bitcast(FP8X4), w1_s[:, cols], w1_bf[:, t, :, :].rearrange("p m j -> p (m j)"))
 
+        for c in range(TILES):
+            picks = offsets[:, c * (P // 16) : (c + 1) * (P // 16)]
+            nc.vector.tensor_copy(xw[:, c * P : (c + 1) * P], xw_all[:].bitcast(U32).indirect(picks))
+
         above = sb.tile([P, TILES, V], F32, name="above", tag="first_in", align_bytes=64)
         for c in range(TILES):
             nc.scalar.activation(above[:, c, :], knot_sb[:], ACT.Relu, bias=thr_cols[:, c : c + 1], scale=-256.0)
 
-        wk_bf = sb.tile([P, V, PACK], BF16, name="wk_bf", tag="stage%d" % (TILES - 1), align_bytes=64)
+        wk_bf = sb.tile([P, V, PACK], BF16, name="wk_bf", tag="weights_bf", align_bytes=64)
         nc.vector.tensor_copy(
             wk_bf[:].rearrange("p (c i) j -> p c j i", i=PACK),
             wk_raw[:].rearrange("p j (c i) -> p c j i", i=PACK),
@@ -99,14 +109,16 @@ def tile_picked_ycard_log_p_kernel(tc, x_words, x_scales, w1, wk, knot, thr, ful
                 )
             h_ps.append(bank)
 
+        hidden = []
+        for c in range(TILES):
+            h_bf = sb.tile([P, P, PACK], BF16, name="h_bf%d" % c, tag="stage%d" % c, align_bytes=64)
+            nc.scalar.activation(h_bf[:], h_ps[c][:].rearrange("p t n -> p n t"), ACT.Relu)
+            hidden.append(h_bf)
+
         grown = sb.tile([P, TILES, V], F32, name="grown")
         z_ps = []
         for c in range(TILES):
-            h_bf = sb.tile([P, P, PACK], BF16, name="h_bf%d" % c, tag="stage%d" % c, align_bytes=64)
-            if c < TILES - 1:
-                nc.scalar.activation(h_bf[:], h_ps[c][:].rearrange("p t n -> p n t"), ACT.Relu)
-            else:
-                nc.vector.tensor_scalar(h_bf[:], h_ps[c][:].rearrange("p t n -> p n t"), 0.0, None, ALU.max)
+            h_bf = hidden[c]
             h_q = sb.tile([P, P], U32, name="h_q%d" % c, tag="codes%d" % c, align_bytes=64)
             h_s = sb.tile([P, P], U8, name="h_s%d" % c, align_bytes=64)
             nc.vector.quantize_mx(h_q[:].bitcast(FP8X4), h_s[:], h_bf[:].rearrange("p n t -> p (n t)"))
@@ -132,7 +144,7 @@ def tile_picked_ycard_log_p_kernel(tc, x_words, x_scales, w1, wk, knot, thr, ful
         soft = []
         for c in range(TILES):
             a = sb.tile([P, V], F32, name="soft%d" % c)
-            nc.scalar.activation(a[:], capped[:, c, :], ACT.Ln, bias=1.0)
+            nc.scalar.activation(a[:], capped[:, c, :], ACT.Ln, bias=one[:])
             soft.append(a)
 
         for c in range(TILES):
@@ -144,5 +156,5 @@ def tile_picked_ycard_log_p_kernel(tc, x_words, x_scales, w1, wk, knot, thr, ful
             factor = sb.tile([P, 1], F32, name="factor%d" % c)
             nc.vector.reciprocal(factor[:], total[:])
             res = sb.tile([P, V], F32, name="res%d" % c)
-            nc.scalar.activation(res[:], piece[:], ACT.Ln, bias=0.1, scale=factor[:])
+            nc.scalar.activation(res[:], piece[:], ACT.Ln, bias=tenth[:], scale=factor[:])
             nc.sync.dma_start(out[c * P : (c + 1) * P, :], res[:])

import math
from contextlib import ExitStack

import concourse.mybir as mybir
from concourse.masks import make_identity

F32 = mybir.dt.float32
BF16 = mybir.dt.bfloat16
I32 = mybir.dt.int32
U32 = mybir.dt.uint32
U16 = mybir.dt.uint16
U8 = mybir.dt.uint8
FP8X4 = mybir.dt.float8_e4m3fn_x4
ALU = mybir.AluOpType
ACT = mybir.ActivationFunctionType

P = 128
PACK = 4
K, T, S, H, V = 512, 1024, 512, 512, 256
TILES = S // P
CAP = 32.0
W1_SPLIT = 44
FLOPS = 2 * K * H * S + 2 * H * S * V


def tile_picked_ycard_log_p_kernel(tc, x_words, x_scales, w1, wk, knot, thr, full, offs, out):
    nc = tc.nc
    with ExitStack() as ctx:
        sb = ctx.enter_context(tc.tile_pool(name="sb", bufs=1))
        ps = ctx.enter_context(tc.psum_pool(name="ps", bufs=1))

        offsets = sb.tile([P, S // 16], U16, name="offsets")
        nc.sync.dma_start(offsets[:], offs)

        one = sb.tile([P, 1], F32, name="one")
        nc.vector.memset(one[:], 1.0)
        tenth = sb.tile([P, 1], F32, name="tenth")
        nc.scalar.activation(tenth[:], one[:], ACT.Copy, scale=0.1)

        xs_all = sb.tile([P, T], U8, name="xs_all", align_bytes=64)
        nc.gpsimd.memset(xs_all[:].bitcast(I32), 0)
        thr_rows = sb.tile([P, P], F32, name="thr_rows")
        nc.gpsimd.memset(thr_rows[:], 0.0)
        identity = sb.tile([P, P], F32, name="identity")
        make_identity(nc, identity[:])

        w1_raw = sb.tile([P, PACK, H], F32, name="w1_raw", tag="first_in", align_bytes=64)
        w1_rows = w1.rearrange("(p j) c -> p j c", j=PACK)
        nc.sync.dma_start(w1_raw[:, 0:2, :], w1_rows[:, 0:2, :])
        for q in range(4):
            nc.sync.dma_start(xs_all[32 * q : 32 * q + 4, :].bitcast(I32), x_scales[0, 4 * q : 4 * q + 4, :].bitcast(I32))
        nc.sync.dma_start(thr_rows[0:TILES, :], thr.rearrange("(c p) o -> c (p o)", p=P))
        nc.sync.dma_start(w1_raw[:, 2:4, :], w1_rows[:, 2:4, :])
        xw_all = sb.tile([P, T], I32, name="xw_all", align_bytes=64)
        nc.sync.dma_start(xw_all[:], x_words[0].rearrange("p n t -> p (n t)").bitcast(I32))
        knot_sb = sb.tile([P, V], F32, name="knot_sb")
        nc.sync.dma_start(knot_sb[:], knot)
        wk_raw = sb.tile([P, PACK, V], F32, name="wk_raw", tag="codes0", align_bytes=64)
        nc.sync.dma_start(wk_raw[:], wk.rearrange("(p j) c -> p j c", j=PACK))
        full_sb = sb.tile([P, V], F32, name="full_sb")
        nc.sync.dma_start(full_sb[:], full)

        xs = sb.tile([P, S], U8, name="xs", align_bytes=64)
        xw = sb.tile([P, S], U32, name="xw", align_bytes=64)
        nc.vector.tensor_copy(xs[:], xs_all[:].indirect(offsets[:]))

        thr_ps = ps.tile([P, P], F32, name="thr_ps", tag="z_ps%d" % (TILES - 1))
        nc.tensor.transpose(thr_ps[:], thr_rows[:], identity[:])
        thr_cols = sb.tile([P, TILES], F32, name="thr_cols")
        nc.scalar.activation(thr_cols[:], thr_ps[:, 0:TILES], ACT.Copy, scale=256.0)

        w1_bf = sb.tile([P, PACK, P, PACK], BF16, name="w1_bf", tag="weights_bf", align_bytes=64)
        dealt = w1_bf[:].rearrange("p t m j -> p m j t")
        rows = w1_raw[:].rearrange("p j (m t) -> p m j t", t=PACK)
        nc.scalar.activation(dealt[:, 0:W1_SPLIT], rows[:, 0:W1_SPLIT], ACT.Copy)
        nc.vector.tensor_copy(dealt[:, W1_SPLIT:P], rows[:, W1_SPLIT:P])
        w1_q = sb.tile([P, H], U32, name="w1_q", align_bytes=64)
        w1_s = sb.tile([P, H], U8, name="w1_s", align_bytes=64)
        for t in range(PACK):
            cols = slice(t * P, (t + 1) * P)
            nc.vector.quantize_mx(w1_q[:, cols].bitcast(FP8X4), w1_s[:, cols], w1_bf[:, t, :, :].rearrange("p m j -> p (m j)"))

        for c in range(TILES):
            picks = offsets[:, c * (P // 16) : (c + 1) * (P // 16)]
            nc.vector.tensor_copy(xw[:, c * P : (c + 1) * P], xw_all[:].bitcast(U32).indirect(picks))

        above = sb.tile([P, TILES, V], F32, name="above", tag="first_in", align_bytes=64)
        for c in range(TILES):
            nc.scalar.activation(above[:, c, :], knot_sb[:], ACT.Relu, bias=thr_cols[:, c : c + 1], scale=-256.0)

        wk_bf = sb.tile([P, V, PACK], BF16, name="wk_bf", tag="weights_bf", align_bytes=64)
        nc.vector.tensor_copy(
            wk_bf[:].rearrange("p (c i) j -> p c j i", i=PACK),
            wk_raw[:].rearrange("p j (c i) -> p c j i", i=PACK),
        )
        wk_q = sb.tile([P, V], U32, name="wk_q", align_bytes=64)
        wk_s = sb.tile([P, V], U8, name="wk_s", align_bytes=64)
        nc.vector.quantize_mx(wk_q[:].bitcast(FP8X4), wk_s[:], wk_bf[:].rearrange("p c j -> p (c j)"))

        h_ps = []
        for c in range(TILES):
            bank = ps.tile([P, PACK, P], F32, name="h_ps%d" % c)
            tok = slice(c * P, (c + 1) * P)
            for t in range(PACK):
                cols = slice(t * P, (t + 1) * P)
                nc.tensor.matmul_mx(
                    bank[:, t, :], lhsT=w1_q[:, cols].bitcast(FP8X4), lhsT_scale=w1_s[:, cols],
                    rhs=xw[:, tok].bitcast(FP8X4), rhs_scale=xs[:, tok], start=True, stop=True,
                )
            h_ps.append(bank)

        hidden = []
        for c in range(TILES):
            h_bf = sb.tile([P, P, PACK], BF16, name="h_bf%d" % c, tag="stage%d" % c, align_bytes=64)
            nc.scalar.activation(h_bf[:], h_ps[c][:].rearrange("p t n -> p n t"), ACT.Relu)
            hidden.append(h_bf)

        grown = sb.tile([P, TILES, V], F32, name="grown")
        z_ps = []
        for c in range(TILES):
            h_bf = hidden[c]
            h_q = sb.tile([P, P], U32, name="h_q%d" % c, tag="codes%d" % c, align_bytes=64)
            h_s = sb.tile([P, P], U8, name="h_s%d" % c, align_bytes=64)
            nc.vector.quantize_mx(h_q[:].bitcast(FP8X4), h_s[:], h_bf[:].rearrange("p n t -> p (n t)"))
            z = ps.tile([P, V], F32, name="z_ps%d" % c, tag="z_ps%d" % c)
            nc.tensor.matmul_mx(
                z[:], lhsT=h_q[:].bitcast(FP8X4), lhsT_scale=h_s[:],
                rhs=wk_q[:].bitcast(FP8X4), rhs_scale=wk_s[:], start=True, stop=True,
            )
            nc.scalar.activation(grown[:, c, :], z[:], ACT.Exp)
            z_ps.append(z)

        capped = sb.tile([P, TILES, V], F32, name="capped")
        nc.vector.tensor_scalar(capped[:], grown[:], math.e**CAP, None, ALU.min)

        reach = []
        for c in range(TILES):
            rr = sb.tile([P, V], F32, name="rr%d" % c, tag="stage%d" % c, align_bytes=64)
            nc.vector.tensor_tensor(rr[:], above[:, c, :], full_sb[:], ALU.min)
            weight = sb.tile([P, V], F32, name="weight%d" % c)
            nc.vector.scalar_tensor_tensor(weight[:], z_ps[c][:], CAP, rr[:], ALU.max, ALU.mult)
            reach.append(weight)

        soft = []
        for c in range(TILES):
            a = sb.tile([P, V], F32, name="soft%d" % c)
            nc.scalar.activation(a[:], capped[:, c, :], ACT.Ln, bias=one[:])
            soft.append(a)

        for c in range(TILES):
            piece = sb.tile([P, V], F32, name="piece%d" % c)
            sums = sb.tile([P, 1], F32, name="sums%d" % c)
            nc.vector.scalar_tensor_tensor(piece[:], soft[c][:], 1.0, reach[c][:], ALU.mult, ALU.mult, accum_out=sums[:])
            total = sb.tile([P, 1], F32, name="total%d" % c)
            nc.vector.tensor_scalar(total[:], sums[:], CAP, 0.01, ALU.add, ALU.mult)
            factor = sb.tile([P, 1], F32, name="factor%d" % c)
            nc.vector.reciprocal(factor[:], total[:])
            res = sb.tile([P, V], F32, name="res%d" % c)
            nc.scalar.activation(res[:], piece[:], ACT.Ln, bias=tenth[:], scale=factor[:])
            nc.sync.dma_start(out[c * P : (c + 1) * P, :], res[:])
